import numpy as np
import ml_dtypes


def mxq(x, axis, fmt="e4m3"):
    dtype, down = {"e4m3": (ml_dtypes.float8_e4m3fn, 7), "e5m2": (ml_dtypes.float8_e5m2, 14)}[fmt]
    v = np.moveaxis(np.asarray(x, np.float32).astype(ml_dtypes.bfloat16).astype(np.float64), axis, -1)
    blocks = v.reshape(v.shape[:-1] + (-1, 32))
    amax = np.abs(blocks).max(-1, keepdims=True)
    byte = np.maximum(np.where(amax > 0, np.frexp(amax)[1] - 1 + 127, 0) - down, 1)
    scale = np.exp2(byte - 127.0)
    codes = (blocks / scale).astype(np.float32).astype(dtype).astype(np.float64)
    return np.moveaxis((codes * scale).reshape(v.shape), -1, axis)


WIDE = False


def mx_kscale(k):
    if not WIDE:
        return np.ones(k)
    levels = np.array([10, -10, 5, -5, 0])
    if k % 512:
        return np.exp2(np.random.permutation(np.resize(levels, k // 32))).repeat(32)
    a = np.empty((k // 512, 16))
    for p in range(k // 512):
        a[p, :8] = np.random.permutation(np.resize(levels, 8))
        for g in range(8):
            far = levels[np.abs(levels - a[p, g]) >= 10]
            a[p, g + 8] = far[np.random.randint(len(far))]
    return np.exp2(a.ravel()).repeat(32)


def f64(x):
    return np.asarray(x).astype(np.float64)


def striped(idx):
    return np.tile(idx.reshape(-1, 16).T, (8, 1)).astype(np.uint16)


def unstriped(offs):
    return offs[:16].T.reshape(-1).astype(np.int64)


def pack_weight(w):
    k, n = w.shape
    w = f64(np.asarray(w, np.float32).astype(ml_dtypes.bfloat16)).reshape(k // 32, 32, n)
    amax = np.abs(w).max(1)
    byte = np.clip(np.where(amax > 0, np.frexp(amax)[1] - 1 + 127 - 7, 1), 1, 254)
    scaled = (w * np.exp2(127.0 - byte)[:, None, :]).reshape(k, n).astype(np.float32)
    words = np.ascontiguousarray(scaled.reshape(k // 512, 128, 4, n).transpose(0, 1, 3, 2)).astype(ml_dtypes.float8_e4m3fn).view(np.uint8)
    return words, np.ascontiguousarray(byte.astype(np.uint8).reshape(k // 512, 16, n))


def unpack_weight(words, scales):
    g, p, n, _ = words.shape
    vals = np.ascontiguousarray(words).view(ml_dtypes.float8_e4m3fn).astype(np.float64) * np.repeat(np.exp2(scales.astype(np.float64) - 127.0), 8, axis=1)[..., None]
    return vals.transpose(0, 1, 3, 2).reshape(g * 512, n)


K, T, S, H, N, W = 512, 1024, 512, 512, 128, 1024
P = 2 ** 7


def setup_inputs():
    n = np.random.standard_normal
    s = mx_kscale(K)[:, None]
    u = mx_kscale(H)
    packed_xT = pack_weight(n((K, T)) * s)
    packed_eT = pack_weight(n((K, W)) * s)
    return {
        "x_words": packed_xT[0],
        "x_scales": packed_xT[1],
        "w1": (n((K, H)) / np.sqrt(K) / s).astype(np.float32),
        "e_words": packed_eT[0],
        "e_scales": packed_eT[1],
        "cond": (np.tile(np.random.uniform(0.7, 1.3, S), (P, 1))).astype(np.float32),
        "across": (np.random.uniform(0.2, 0.9, (H, 1))).astype(np.float32),
        "within": (np.random.uniform(0.05, 0.4, (H, 1))).astype(np.float32),
        "unit": (np.random.uniform(0.5, 1.5, (H, 1)) * u[:, None]).astype(np.float32),
        "wo": (n((H, N)) / np.sqrt(H) / u[:, None]).astype(np.float32),
        "offs": striped(np.random.permutation(T)[:S]),
        "test": striped(np.random.permutation(W)[:S]),
    }


def reference(x_words, x_scales, w1, e_words, e_scales, cond, across, within, unit, wo, offs, test):
    xq = unpack_weight(x_words, x_scales)[:, unstriped(offs)]
    w1q = mxq(f64(w1), 0, "e4m3")
    pa = w1q.T @ xq
    e_test = unpack_weight(e_words, e_scales)[:, unstriped(test)]
    pb = w1q.T @ e_test
    pc = pb * f64(cond)[:1]
    qd = f64(across) * (pa * pc) - (0.5 * (f64(within) * ((pa) ** 2 + (pc) ** 2)))
    zz = f64(unit) * qd
    return mxq(f64(wo), 0, "e4m3").T @ mxq(zz, 0, "e4m3")

@@ -1,0 +1,182 @@
+from contextlib import ExitStack
+
+import concourse.mybir as mybir
+from concourse.masks import make_identity
+
+F32 = mybir.dt.float32
+BF16 = mybir.dt.bfloat16
+I32 = mybir.dt.int32
+U32 = mybir.dt.uint32
+U16 = mybir.dt.uint16
+U8 = mybir.dt.uint8
+FP8X4 = mybir.dt.float8_e4m3fn_x4
+ALU = mybir.AluOpType
+ACT = mybir.ActivationFunctionType
+
+P = 128
+K, T, S, H, N = 512, 1024, 512, 512, 128
+FLOPS = 2 * K * H * S * 2 + 2 * H * N * S
+HALF = S // 2
+
+
+def tile_picked_yplda_quad_p_kernel(
+    tc, x_words, x_scales, w1, e_words, e_scales, cond, across, within, unit, wo, offs, test, out
+):
+    nc = tc.nc
+    with ExitStack() as ctx:
+        sb = ctx.enter_context(tc.tile_pool(name="sb", bufs=1))
+        ps = ctx.enter_context(tc.psum_pool(name="ps", bufs=1))
+        reuse = ctx.enter_context(tc.tile_pool(name="reuse", bufs=1))
+
+        offs_t = sb.tile([P, S // 16], U16, name="offs_t")
+        test_t = sb.tile([P, S // 16], U16, name="test_t")
+        xw_win = sb.tile([P, T], I32, name="xw_win", align_bytes=64)
+        ew_win = sb.tile([P, T], I32, name="ew_win", align_bytes=64)
+        xs_win = sb.tile([P, T], U8, name="xs_win", align_bytes=64)
+        es_win = sb.tile([P, T], U8, name="es_win", align_bytes=64)
+        w1_raw = [sb.tile([P, 4, H // 2], F32, name=f"w1_raw{u}") for u in range(2)]
+        wo_raw = sb.tile([P, 4, N], F32, name="wo_raw")
+        a_t = sb.tile([P, 4], F32, name="a_t")
+        w_t = sb.tile([P, 4], F32, name="w_t")
+        u_t = sb.tile([P, 4], F32, name="u_t")
+        c_t = sb.tile([P, 4], F32, name="c_t")
+
+        def load_scales(win, src):
+            for q in range(4):
+                rows = src[0:1, 4 * q : 4 * q + 4, :].bitcast(I32)
+                nc.sync.dma_start(win[32 * q : 32 * q + 32, :].bitcast(I32), rows.broadcast_to([8, 4, T // 4]))
+
+        nc.sync.dma_start(ew_win[:], e_words[0].rearrange("p n t -> p (n t)").bitcast(I32))
+        nc.sync.dma_start(test_t[:], test)
+        load_scales(es_win, e_scales)
+        w1v = w1.rearrange("(p j) c -> p j c", j=4)
+        for u in range(2):
+            nc.sync.dma_start(w1_raw[u][:], w1v[:, :, u * 256 : (u + 1) * 256])
+        nc.sync.dma_start(xw_win[:], x_words[0].rearrange("p n t -> p (n t)").bitcast(I32))
+        nc.sync.dma_start(offs_t[:], offs)
+        load_scales(xs_win, x_scales)
+        with nc.allow_non_contiguous_dma(reason="one factor a pair, pairs on the partitions"):
+            nc.sync.dma_start(c_t[:], cond[0:1, :].rearrange("o (g p) -> p (o g)", p=P))
+        for tl, src in ((a_t, across), (u_t, unit), (w_t, within)):
+            nc.gpsimd.dma_start(tl[:], src.rearrange("(p t) o -> p (t o)", t=4))
+        nc.sync.dma_start(wo_raw[:], wo.rearrange("(p j) n -> p j n", j=4))
+
+        cross = sb.tile([P, 4], F32, name="cross")
+        nsq = sb.tile([P, 4], F32, name="nsq")
+        ident = sb.tile([P, P], F32, name="ident")
+        make_identity(nc, ident[:])
+
+        def gather(name, words, scales, lst, h, base):
+            g_w = reuse.tile([P, HALF], U32, name=f"{name}_w{h}", align_bytes=64, offset=base + h * 2048)
+            g_s = reuse.tile([P, HALF], U8, name=f"{name}_s{h}", align_bytes=64, offset=base + h * 2048 + 1024)
+            part = lst[:, h * 16 : (h + 1) * 16]
+            nc.vector.tensor_copy(g_w[:], words[:].bitcast(U32).indirect(part))
+            nc.vector.tensor_copy(g_s[:], scales[:].indirect(part))
+            return g_w, g_s
+
+        eg = [gather("eg", ew_win, es_win, test_t, h, 4096) for h in range(2)]
+
+        nc.vector.tensor_tensor(cross[:], u_t[:], a_t[:], ALU.mult)
+        nc.vector.scalar_tensor_tensor(nsq[:], u_t[:], -0.5, w_t[:], ALU.mult, ALU.mult)
+        w1_b = reuse.tile([P, 4, P, 4], BF16, name="w1_b", align_bytes=64, offset=0)
+
+        def cast_w1(copy, u, m0, m1):
+            src = w1_raw[u][:, :, 4 * m0 : 4 * m1].rearrange("p j (m t) -> p m j t", t=4)
+            dst = w1_b[:, :, 64 * u + m0 : 64 * u + m1, :].rearrange("p t m j -> p m j t")
+            copy(dst, src)
+
+        cast_w1(nc.scalar.copy, 0, 0, 64)
+        cast_w1(nc.scalar.copy, 1, 0, 20)
+        cast_w1(nc.vector.tensor_copy, 1, 20, 64)
+        w1_c = sb.tile([P, H], U32, name="w1_c", align_bytes=64)
+        w1_s = sb.tile([P, H], U8, name="w1_s", align_bytes=64)
+        nc.vector.quantize_mx(out=w1_c[:].bitcast(FP8X4), scales=w1_s[:], in_=w1_b[:].rearrange("p t m j -> p (t m j)"))
+
+        xg = [gather("xg", xw_win, xs_win, offs_t, h, 0) for h in range(2)]
+
+        wo_b = sb.tile([P, N, 4], BF16, name="wo_b", align_bytes=64)
+        nc.gpsimd.tensor_copy(wo_b[:], wo_raw[:].rearrange("p j n -> p n j"))
+        wo_c = sb.tile([P, N], U32, name="wo_c", align_bytes=64)
+        wo_s = sb.tile([P, N], U8, name="wo_s", align_bytes=64)
+
+        def front(h):
+            eg_w, eg_s = eg[h]
+            xg_w, xg_s = xg[h]
+            yT = []
+            for g in range(2):
+                pb = ps.tile([P, H], F32, name=f"pb{h}{g}", tag="pb", bufs=2)
+                cols = slice(P * g, P * (g + 1))
+                nc.tensor.matmul_mx(out=pb[:], lhsT=eg_w[:, cols].bitcast(FP8X4), lhsT_scale=eg_s[:, cols],
+                                    rhs=w1_c[:].bitcast(FP8X4), rhs_scale=w1_s[:], start=True, stop=True)
+                y_sb = sb.tile([P, H], F32, name=f"yT{h}{g}")
+                nc.scalar.activation(y_sb[:], pb[:], ACT.Copy, scale=c_t[:, 2 * h + g : 2 * h + g + 1])
+                yT.append(y_sb)
+            pa = []
+            for u in range(2):
+                bank = ps.tile([P, 2, HALF], F32, name=f"pa{h}{u}", tag=f"pa{h}", bufs=2)
+                for tt in range(2):
+                    cols = slice(P * (2 * u + tt), P * (2 * u + tt + 1))
+                    nc.tensor.matmul_mx(out=bank[:, tt, :], lhsT=w1_c[:, cols].bitcast(FP8X4), lhsT_scale=w1_s[:, cols],
+                                        rhs=xg_w[:].bitcast(FP8X4), rhs_scale=xg_s[:], start=True, stop=True)
+                pa.append(bank)
+            ax = sb.tile([P, 4, HALF], F32, name=f"ax{h}")
+            hx = sb.tile([P, 4, HALF], F32, name=f"hx{h}")
+            x2 = sb.tile([P, 4, HALF], F32, name=f"x2{h}")
+            for t in range(4):
+                nc.scalar.activation(ax[:, t, :], pa[t // 2][:, t % 2, :], ACT.Copy, scale=cross[:, t : t + 1])
+            for u in range(2):
+                nc.scalar.activation(x2[:, 2 * u : 2 * u + 2, :], pa[u][:], ACT.Square)
+                for t in (2 * u, 2 * u + 1):
+                    nc.gpsimd.tensor_scalar(hx[:, t, :], x2[:, t, :], nsq[:, t : t + 1], 0.0, ALU.mult, ALU.add)
+            y = []
+            for u in range(2):
+                bank = ps.tile([P, 2, HALF], F32, name=f"y{h}{u}", tag="y" if h == 0 else "pa0", bufs=2)
+                for g in range(2):
+                    for tt in range(2):
+                        t = 2 * u + tt
+                        nc.tensor.transpose(bank[:, tt, P * g : P * (g + 1)], yT[g][:, P * t : P * (t + 1)], ident[:])
+                y.append(bank)
+            return ax, hx, y
+
+        fronts = [front(h) for h in range(2)]
+
+        def products(h):
+            ax, hx, y = fronts[h]
+            lin = sb.tile([P, 4, HALF], F32, name=f"lin{h}")
+            prod = sb.tile([P, 4, HALF], F32, name=f"prod{h}")
+            for t in range(4):
+                nc.vector.scalar_tensor_tensor(lin[:, t, :], y[t // 2][:, t % 2, :], nsq[:, t : t + 1], ax[:, t, :], ALU.mult, ALU.add)
+            for u in range(2):
+                nc.vector.tensor_tensor(prod[:, 2 * u : 2 * u + 2, :], y[u][:], lin[:, 2 * u : 2 * u + 2, :], ALU.mult)
+            return prod
+
+        def rounded(h, prod, j0, n):
+            hx = fronts[h][1]
+            zz = sb.tile([P, n, 4], BF16, name=f"zz{h}_{j0}", align_bytes=64)
+            nc.vector.tensor_tensor(
+                zz[:].rearrange("p (c i) t -> p c t i", i=4),
+                prod[:, :, j0 : j0 + n].rearrange("p t (c i) -> p c t i", i=4),
+                hx[:, :, j0 : j0 + n].rearrange("p t (c i) -> p c t i", i=4),
+                ALU.add,
+            )
+            return zz
+
+        def finish(h, zz, j0, n, tag):
+            zz_c = sb.tile([P, n], U32, name=f"zz_c{h}_{j0}", align_bytes=64)
+            zz_s = sb.tile([P, n], U8, name=f"zz_s{h}_{j0}", align_bytes=64)
+            nc.vector.quantize_mx(out=zz_c[:].bitcast(FP8X4), scales=zz_s[:], in_=zz[:].rearrange("p j t -> p (j t)"))
+            acc = ps.tile([P, n], F32, name=f"acc{h}_{j0}", tag=tag, bufs=2)
+            nc.tensor.matmul_mx(out=acc[:], lhsT=wo_c[:].bitcast(FP8X4), lhsT_scale=wo_s[:],
+                                rhs=zz_c[:].bitcast(FP8X4), rhs_scale=zz_s[:], start=True, stop=True)
+            res = sb.tile([P, n], F32, name=f"res{h}_{j0}")
+            nc.scalar.copy(res[:], acc[:])
+            nc.sync.dma_start(out[:, h * HALF + j0 : h * HALF + j0 + n], res[:])
+
+        prod0 = products(0)
+        zz0 = rounded(0, prod0, 0, HALF)
+        nc.vector.quantize_mx(out=wo_c[:].bitcast(FP8X4), scales=wo_s[:], in_=wo_b[:].rearrange("p n j -> p (n j)"))
+        finish(0, zz0, 0, HALF, "y")
+        prod1 = products(1)
+        zz1 = [rounded(1, prod1, j0, P) for j0 in (0, P)]
+        finish(1, zz1[0], 0, P, "y")
+        finish(1, zz1[1], P, P, "pb")

@@ -52,19 +52,33 @@ def tile_picked_yplda_quad_p_kernel(
         w1v = w1.rearrange("(p j) c -> p j c", j=4)
         for u in range(2):
             nc.sync.dma_start(w1_raw[u][:], w1v[:, :, u * 256 : (u + 1) * 256])
+        c_rows = sb.tile([P, P], F32, name="c_rows")
+        nc.sync.dma_start(c_rows[:], cond[0:32, :].rearrange("r (g j) -> (r g) j", j=P))
         nc.sync.dma_start(xw_win[:], x_words[0].rearrange("p n t -> p (n t)").bitcast(I32))
         nc.sync.dma_start(offs_t[:], offs)
         load_scales(xs_win, x_scales)
-        with nc.allow_non_contiguous_dma(reason="one factor a pair, pairs on the partitions"):
-            nc.sync.dma_start(c_t[:], cond[0:1, :].rearrange("o (g p) -> p (o g)", p=P))
-        for tl, src in ((a_t, across), (u_t, unit), (w_t, within)):
+        for tl, src in ((u_t, unit), (w_t, within), (a_t, across)):
             nc.gpsimd.dma_start(tl[:], src.rearrange("(p t) o -> p (t o)", t=4))
         nc.sync.dma_start(wo_raw[:], wo.rearrange("(p j) n -> p j n", j=4))
 
         cross = sb.tile([P, 4], F32, name="cross")
+        uw = sb.tile([P, 4], F32, name="uw")
         nsq = sb.tile([P, 4], F32, name="nsq")
         ident = sb.tile([P, P], F32, name="ident")
         make_identity(nc, ident[:])
+        ua = sb.tile([P, 4], F32, name="ua")
+        ua2 = sb.tile([P, 4], F32, name="ua2")
+        s5 = sb.tile([P, 4], F32, name="s5")
+        root = sb.tile([P, 4], F32, name="root")
+        half = sb.tile([P, 4], F32, name="half")
+        nc.gpsimd.memset(half[:], 0.5)
+        nc.gpsimd.tensor_tensor(uw[:], u_t[:], w_t[:], ALU.mult)
+        nc.gpsimd.tensor_scalar(s5[:], uw[:], 0.0, -0.5, ALU.is_ge, ALU.add)
+        nc.gpsimd.tensor_tensor(ua[:], u_t[:], a_t[:], ALU.mult)
+        nc.gpsimd.tensor_scalar(ua2[:], s5[:], -2.0, 0.0, ALU.mult, ALU.add)
+        nc.gpsimd.tensor_tensor(nsq[:], uw[:], s5[:], ALU.mult)
+        nc.gpsimd.tensor_tensor(cross[:], ua[:], ua2[:], ALU.mult)
+        nc.gpsimd.tensor_tensor(root[:], nsq[:], half[:], ALU.pow)
 
         def gather(name, words, scales, lst, h, base):
             g_w = reuse.tile([P, HALF], U32, name=f"{name}_w{h}", align_bytes=64, offset=base + h * 2048)
@@ -74,10 +88,12 @@ def tile_picked_yplda_quad_p_kernel(
             nc.vector.tensor_copy(g_s[:], scales[:].indirect(part))
             return g_w, g_s
 
-        eg = [gather("eg", ew_win, es_win, test_t, h, 4096) for h in range(2)]
+        eg_words = sb.tile([P, S], U32, name="eg_words", align_bytes=64)
+        eg_scales = sb.tile([P, S], U8, name="eg_scales", align_bytes=64)
+        nc.vector.tensor_copy(eg_words[:], ew_win[:].bitcast(U32).indirect(test_t[:]))
+        nc.vector.tensor_copy(eg_scales[:], es_win[:].indirect(test_t[:]))
+        eg = [(eg_words[:, h * HALF : (h + 1) * HALF], eg_scales[:, h * HALF : (h + 1) * HALF]) for h in range(2)]
 
-        nc.vector.tensor_tensor(cross[:], u_t[:], a_t[:], ALU.mult)
-        nc.vector.scalar_tensor_tensor(nsq[:], u_t[:], -0.5, w_t[:], ALU.mult, ALU.mult)
         w1_b = reuse.tile([P, 4, P, 4], BF16, name="w1_b", align_bytes=64, offset=0)
 
         def cast_w1(copy, u, m0, m1):
@@ -88,6 +104,9 @@ def tile_picked_yplda_quad_p_kernel(
         cast_w1(nc.scalar.copy, 0, 0, 64)
         cast_w1(nc.scalar.copy, 1, 0, 20)
         cast_w1(nc.vector.tensor_copy, 1, 20, 64)
+        c_bank = ps.tile([P, P], F32, name="c_bank", tag="pb", bufs=2)
+        nc.tensor.transpose(c_bank[:], c_rows[:], ident[:])
+        nc.scalar.copy(c_t[:], c_bank[:, 0:4])
         w1_c = sb.tile([P, H], U32, name="w1_c", align_bytes=64)
         w1_s = sb.tile([P, H], U8, name="w1_s", align_bytes=64)
         nc.vector.quantize_mx(out=w1_c[:].bitcast(FP8X4), scales=w1_s[:], in_=w1_b[:].rearrange("p t m j -> p (t m j)"))
@@ -95,9 +114,16 @@ def tile_picked_yplda_quad_p_kernel(
         xg = [gather("xg", xw_win, xs_win, offs_t, h, 0) for h in range(2)]
 
         wo_b = sb.tile([P, N, 4], BF16, name="wo_b", align_bytes=64)
-        nc.gpsimd.tensor_copy(wo_b[:], wo_raw[:].rearrange("p j n -> p n j"))
         wo_c = sb.tile([P, N], U32, name="wo_c", align_bytes=64)
         wo_s = sb.tile([P, N], U8, name="wo_s", align_bytes=64)
+
+        nc.vector.tensor_tensor(
+            wo_b[:].rearrange("p (c i) j -> p c j i", i=4),
+            wo_raw[:].rearrange("p j (c i) -> p c j i", i=4),
+            ua2[:].unsqueeze(1).unsqueeze(3).broadcast_to([P, N // 4, 4, 4]),
+            ALU.mult,
+        )
+        nc.vector.quantize_mx(out=wo_c[:].bitcast(FP8X4), scales=wo_s[:], in_=wo_b[:].rearrange("p n j -> p (n j)"))
 
         def front(h):
             eg_w, eg_s = eg[h]
@@ -121,13 +147,10 @@ def tile_picked_yplda_quad_p_kernel(
                 pa.append(bank)
             ax = sb.tile([P, 4, HALF], F32, name=f"ax{h}")
             hx = sb.tile([P, 4, HALF], F32, name=f"hx{h}")
-            x2 = sb.tile([P, 4, HALF], F32, name=f"x2{h}")
             for t in range(4):
                 nc.scalar.activation(ax[:, t, :], pa[t // 2][:, t % 2, :], ACT.Copy, scale=cross[:, t : t + 1])
-            for u in range(2):
-                nc.scalar.activation(x2[:, 2 * u : 2 * u + 2, :], pa[u][:], ACT.Square)
-                for t in (2 * u, 2 * u + 1):
-                    nc.gpsimd.tensor_scalar(hx[:, t, :], x2[:, t, :], nsq[:, t : t + 1], 0.0, ALU.mult, ALU.add)
+            for t in range(4):
+                nc.scalar.activation(hx[:, t, :], pa[t // 2][:, t % 2, :], ACT.Square, scale=root[:, t : t + 1])
             y = []
             for u in range(2):
                 bank = ps.tile([P, 2, HALF], F32, name=f"y{h}{u}", tag="y" if h == 0 else "pa0", bufs=2)
@@ -174,7 +197,6 @@ def tile_picked_yplda_quad_p_kernel(
 
         prod0 = products(0)
         zz0 = rounded(0, prod0, 0, HALF)
-        nc.vector.quantize_mx(out=wo_c[:].bitcast(FP8X4), scales=wo_s[:], in_=wo_b[:].rearrange("p n j -> p (n j)"))
         finish(0, zz0, 0, HALF, "y")
         prod1 = products(1)
         zz1 = [rounded(1, prod1, j0, P) for j0 in (0, P)]

@@ -46,20 +46,22 @@ def tile_picked_yplda_quad_p_kernel(
                 rows = src[0:1, 4 * q : 4 * q + 4, :].bitcast(I32)
                 nc.sync.dma_start(win[32 * q : 32 * q + 32, :].bitcast(I32), rows.broadcast_to([8, 4, T // 4]))
 
-        nc.sync.dma_start(ew_win[:], e_words[0].rearrange("p n t -> p (n t)").bitcast(I32))
+        nc.gpsimd.memset(xs_win[:].bitcast(I32), 0)
+        w1v = w1.rearrange("(p j) c -> p j c", j=4)
+        nc.sync.dma_start(w1_raw[0][:], w1v[:, :, 0:256])
         nc.sync.dma_start(test_t[:], test)
         load_scales(es_win, e_scales)
-        w1v = w1.rearrange("(p j) c -> p j c", j=4)
-        for u in range(2):
-            nc.sync.dma_start(w1_raw[u][:], w1v[:, :, u * 256 : (u + 1) * 256])
-        c_rows = sb.tile([P, P], F32, name="c_rows")
-        nc.sync.dma_start(c_rows[:], cond[0:32, :].rearrange("r (g j) -> (r g) j", j=P))
+        nc.sync.dma_start(w1_raw[1][:], w1v[:, :, 256:512])
+        nc.sync.dma_start(ew_win[:], e_words[0].rearrange("p n t -> p (n t)").bitcast(I32))
         nc.sync.dma_start(xw_win[:], x_words[0].rearrange("p n t -> p (n t)").bitcast(I32))
         nc.sync.dma_start(offs_t[:], offs)
-        load_scales(xs_win, x_scales)
+        c_rows = sb.tile([P, P], F32, name="c_rows")
+        nc.sync.dma_start(c_rows[:], cond[0:32, :].rearrange("r (g j) -> (r g) j", j=P))
+        for q in range(4):
+            nc.sync.dma_start(xs_win[32 * q : 32 * q + 4, :].bitcast(I32), x_scales[0, 4 * q : 4 * q + 4, :].bitcast(I32))
+        nc.sync.dma_start(wo_raw[:], wo.rearrange("(p j) n -> p j n", j=4))
         for tl, src in ((u_t, unit), (w_t, within), (a_t, across)):
             nc.gpsimd.dma_start(tl[:], src.rearrange("(p t) o -> p (t o)", t=4))
-        nc.sync.dma_start(wo_raw[:], wo.rearrange("(p j) n -> p j n", j=4))
 
         cross = sb.tile([P, 4], F32, name="cross")
         uw = sb.tile([P, 4], F32, name="uw")
@@ -80,19 +82,17 @@ def tile_picked_yplda_quad_p_kernel(
         nc.gpsimd.tensor_tensor(cross[:], ua[:], ua2[:], ALU.mult)
         nc.gpsimd.tensor_tensor(root[:], nsq[:], half[:], ALU.pow)
 
-        def gather(name, words, scales, lst, h, base):
-            g_w = reuse.tile([P, HALF], U32, name=f"{name}_w{h}", align_bytes=64, offset=base + h * 2048)
-            g_s = reuse.tile([P, HALF], U8, name=f"{name}_s{h}", align_bytes=64, offset=base + h * 2048 + 1024)
-            part = lst[:, h * 16 : (h + 1) * 16]
-            nc.vector.tensor_copy(g_w[:], words[:].bitcast(U32).indirect(part))
-            nc.vector.tensor_copy(g_s[:], scales[:].indirect(part))
-            return g_w, g_s
+        def gather_scales(name, win, lst):
+            g_s = sb.tile([P, S], U8, name=name, align_bytes=64)
+            nc.vector.tensor_copy(g_s[:], win[:].indirect(lst[:]))
+            return g_s
 
-        eg_words = sb.tile([P, S], U32, name="eg_words", align_bytes=64)
-        eg_scales = sb.tile([P, S], U8, name="eg_scales", align_bytes=64)
-        nc.vector.tensor_copy(eg_words[:], ew_win[:].bitcast(U32).indirect(test_t[:]))
-        nc.vector.tensor_copy(eg_scales[:], es_win[:].indirect(test_t[:]))
-        eg = [(eg_words[:, h * HALF : (h + 1) * HALF], eg_scales[:, h * HALF : (h + 1) * HALF]) for h in range(2)]
+        def gather_words(name, win, lst, h, base):
+            g_w = reuse.tile([P, HALF], U32, name=f"{name}{h}", align_bytes=64, offset=base)
+            nc.vector.tensor_copy(g_w[:], win[:].bitcast(U32).indirect(lst[:, h * 16 : (h + 1) * 16]))
+            return g_w
+
+        eg_sc = gather_scales("eg_s", es_win, test_t)
 
         w1_b = reuse.tile([P, 4, P, 4], BF16, name="w1_b", align_bytes=64, offset=0)
 
@@ -104,26 +104,25 @@ def tile_picked_yplda_quad_p_kernel(
         cast_w1(nc.scalar.copy, 0, 0, 64)
         cast_w1(nc.scalar.copy, 1, 0, 20)
         cast_w1(nc.vector.tensor_copy, 1, 20, 64)
-        c_bank = ps.tile([P, P], F32, name="c_bank", tag="pb", bufs=2)
+        c_bank = ps.tile([P, P], F32, name="c_bank", tag="y", bufs=2)
         nc.tensor.transpose(c_bank[:], c_rows[:], ident[:])
         nc.scalar.copy(c_t[:], c_bank[:, 0:4])
         w1_c = sb.tile([P, H], U32, name="w1_c", align_bytes=64)
         w1_s = sb.tile([P, H], U8, name="w1_s", align_bytes=64)
         nc.vector.quantize_mx(out=w1_c[:].bitcast(FP8X4), scales=w1_s[:], in_=w1_b[:].rearrange("p t m j -> p (t m j)"))
 
-        xg = [gather("xg", xw_win, xs_win, offs_t, h, 0) for h in range(2)]
+        eg = [(gather_words("eg_w", ew_win, test_t, h, 1024 * h), eg_sc[:, h * HALF : (h + 1) * HALF]) for h in range(2)]
+        xg = []
+        for h in range(2):
+            words = gather_words("xg_w", xw_win, offs_t, h, 2048 + 1024 * h)
+            g_s = sb.tile([P, HALF], U8, name=f"xg_s{h}", align_bytes=64)
+            nc.vector.tensor_copy(g_s[:], xs_win[:].indirect(offs_t[:, h * 16 : (h + 1) * 16]))
+            xg.append((words, g_s[:]))
 
         wo_b = sb.tile([P, N, 4], BF16, name="wo_b", align_bytes=64)
         wo_c = sb.tile([P, N], U32, name="wo_c", align_bytes=64)
         wo_s = sb.tile([P, N], U8, name="wo_s", align_bytes=64)
 
-        nc.vector.tensor_tensor(
-            wo_b[:].rearrange("p (c i) j -> p c j i", i=4),
-            wo_raw[:].rearrange("p j (c i) -> p c j i", i=4),
-            ua2[:].unsqueeze(1).unsqueeze(3).broadcast_to([P, N // 4, 4, 4]),
-            ALU.mult,
-        )
-        nc.vector.quantize_mx(out=wo_c[:].bitcast(FP8X4), scales=wo_s[:], in_=wo_b[:].rearrange("p n j -> p (n j)"))
 
         def front(h):
             eg_w, eg_s = eg[h]
@@ -134,7 +133,7 @@ def tile_picked_yplda_quad_p_kernel(
                 cols = slice(P * g, P * (g + 1))
                 nc.tensor.matmul_mx(out=pb[:], lhsT=eg_w[:, cols].bitcast(FP8X4), lhsT_scale=eg_s[:, cols],
                                     rhs=w1_c[:].bitcast(FP8X4), rhs_scale=w1_s[:], start=True, stop=True)
-                y_sb = sb.tile([P, H], F32, name=f"yT{h}{g}")
+                y_sb = reuse.tile([P, H], F32, name=f"yT{h}{g}", align_bytes=64, offset=4096 + 2048 * (2 * h + g))
                 nc.scalar.activation(y_sb[:], pb[:], ACT.Copy, scale=c_t[:, 2 * h + g : 2 * h + g + 1])
                 yT.append(y_sb)
             pa = []
@@ -143,7 +142,7 @@ def tile_picked_yplda_quad_p_kernel(
                 for tt in range(2):
                     cols = slice(P * (2 * u + tt), P * (2 * u + tt + 1))
                     nc.tensor.matmul_mx(out=bank[:, tt, :], lhsT=w1_c[:, cols].bitcast(FP8X4), lhsT_scale=w1_s[:, cols],
-                                        rhs=xg_w[:].bitcast(FP8X4), rhs_scale=xg_s[:], start=True, stop=True)
+                                        rhs=xg_w[:].bitcast(FP8X4), rhs_scale=xg_s, start=True, stop=True)
                 pa.append(bank)
             ax = sb.tile([P, 4, HALF], F32, name=f"ax{h}")
             hx = sb.tile([P, 4, HALF], F32, name=f"hx{h}")
@@ -162,13 +161,21 @@ def tile_picked_yplda_quad_p_kernel(
             return ax, hx, y
 
         fronts = [front(h) for h in range(2)]
+        wo_sg = reuse.tile([P, 4, N], F32, name="wo_sg", align_bytes=64, offset=4096 + 2048 * 3)
+        for j in range(4):
+            nc.scalar.activation(wo_sg[:, j, :], wo_raw[:, j, :], ACT.Copy, scale=ua2[:, j : j + 1])
+        nc.scalar.copy(wo_b[:].rearrange("p (c i) j -> p c j i", i=4), wo_sg[:].rearrange("p j (c i) -> p c j i", i=4))
 
-        def products(h):
+        def linear(h):
             ax, hx, y = fronts[h]
             lin = sb.tile([P, 4, HALF], F32, name=f"lin{h}")
-            prod = sb.tile([P, 4, HALF], F32, name=f"prod{h}")
             for t in range(4):
                 nc.vector.scalar_tensor_tensor(lin[:, t, :], y[t // 2][:, t % 2, :], nsq[:, t : t + 1], ax[:, t, :], ALU.mult, ALU.add)
+            return lin
+
+        def products(h, lin):
+            y = fronts[h][2]
+            prod = sb.tile([P, 4, HALF], F32, name=f"prod{h}")
             for u in range(2):
                 nc.vector.tensor_tensor(prod[:, 2 * u : 2 * u + 2, :], y[u][:], lin[:, 2 * u : 2 * u + 2, :], ALU.mult)
             return prod
@@ -184,21 +191,27 @@ def tile_picked_yplda_quad_p_kernel(
             )
             return zz
 
-        def finish(h, zz, j0, n, tag):
+        def quantised(h, zz, j0, n):
             zz_c = sb.tile([P, n], U32, name=f"zz_c{h}_{j0}", align_bytes=64)
             zz_s = sb.tile([P, n], U8, name=f"zz_s{h}_{j0}", align_bytes=64)
             nc.vector.quantize_mx(out=zz_c[:].bitcast(FP8X4), scales=zz_s[:], in_=zz[:].rearrange("p j t -> p (j t)"))
+            return zz_c, zz_s
+
+        def finish(h, zq, j0, n, tag, queue):
             acc = ps.tile([P, n], F32, name=f"acc{h}_{j0}", tag=tag, bufs=2)
             nc.tensor.matmul_mx(out=acc[:], lhsT=wo_c[:].bitcast(FP8X4), lhsT_scale=wo_s[:],
-                                rhs=zz_c[:].bitcast(FP8X4), rhs_scale=zz_s[:], start=True, stop=True)
+                                rhs=zq[0][:].bitcast(FP8X4), rhs_scale=zq[1][:], start=True, stop=True)
             res = sb.tile([P, n], F32, name=f"res{h}_{j0}")
             nc.scalar.copy(res[:], acc[:])
-            nc.sync.dma_start(out[:, h * HALF + j0 : h * HALF + j0 + n], res[:])
+            queue.dma_start(out[:, h * HALF + j0 : h * HALF + j0 + n], res[:])
 
-        prod0 = products(0)
+        prod0 = products(0, linear(0))
         zz0 = rounded(0, prod0, 0, HALF)
-        finish(0, zz0, 0, HALF, "y")
-        prod1 = products(1)
-        zz1 = [rounded(1, prod1, j0, P) for j0 in (0, P)]
-        finish(1, zz1[0], 0, P, "y")
-        finish(1, zz1[1], P, P, "pb")
+        prod1 = products(1, linear(1))
+        zq0 = quantised(0, zz0, 0, HALF)
+        zz1a = rounded(1, prod1, 0, P)
+        nc.vector.quantize_mx(out=wo_c[:].bitcast(FP8X4), scales=wo_s[:], in_=wo_b[:].rearrange("p n j -> p (n j)"))
+        finish(0, zq0, 0, HALF, "y", nc.sync)
+        zz1b = rounded(1, prod1, P, P)
+        finish(1, quantised(1, zz1a, 0, P), 0, P, "y", nc.sync)
+        finish(1, quantised(1, zz1b, P, P), P, P, "pb", nc.scalar)

@@ -55,8 +55,8 @@ def tile_picked_yplda_quad_p_kernel(
         nc.sync.dma_start(ew_win[:], e_words[0].rearrange("p n t -> p (n t)").bitcast(I32))
         nc.sync.dma_start(xw_win[:], x_words[0].rearrange("p n t -> p (n t)").bitcast(I32))
         nc.sync.dma_start(offs_t[:], offs)
-        c_rows = sb.tile([P, P], F32, name="c_rows")
-        nc.sync.dma_start(c_rows[:], cond[0:32, :].rearrange("r (g j) -> (r g) j", j=P))
+        with nc.allow_non_contiguous_dma(reason="one factor a pair, pairs on the partitions"):
+            nc.sync.dma_start(c_t[:], cond[0:1, :].rearrange("o (g p) -> p (o g)", p=P))
         for q in range(4):
             nc.sync.dma_start(xs_win[32 * q : 32 * q + 4, :].bitcast(I32), x_scales[0, 4 * q : 4 * q + 4, :].bitcast(I32))
         nc.sync.dma_start(wo_raw[:], wo.rearrange("(p j) n -> p j n", j=4))
@@ -104,9 +104,6 @@ def tile_picked_yplda_quad_p_kernel(
         cast_w1(nc.scalar.copy, 0, 0, 64)
         cast_w1(nc.scalar.copy, 1, 0, 20)
         cast_w1(nc.vector.tensor_copy, 1, 20, 64)
-        c_bank = ps.tile([P, P], F32, name="c_bank", tag="y", bufs=2)
-        nc.tensor.transpose(c_bank[:], c_rows[:], ident[:])
-        nc.scalar.copy(c_t[:], c_bank[:, 0:4])
         w1_c = sb.tile([P, H], U32, name="w1_c", align_bytes=64)
         w1_s = sb.tile([P, H], U8, name="w1_s", align_bytes=64)
         nc.vector.quantize_mx(out=w1_c[:].bitcast(FP8X4), scales=w1_s[:], in_=w1_b[:].rearrange("p t m j -> p (t m j)"))
@@ -127,37 +124,37 @@ def tile_picked_yplda_quad_p_kernel(
         def front(h):
             eg_w, eg_s = eg[h]
             xg_w, xg_s = xg[h]
+            pb_tags, pa_tags, y_tags = (("AB", "CB", "DE"), ("AF", "GH", "CA"))[h]
             yT = []
             for g in range(2):
-                pb = ps.tile([P, H], F32, name=f"pb{h}{g}", tag="pb", bufs=2)
+                pb = ps.tile([P, H], F32, name=f"pb{h}{g}", tag=pb_tags[g])
                 cols = slice(P * g, P * (g + 1))
                 nc.tensor.matmul_mx(out=pb[:], lhsT=eg_w[:, cols].bitcast(FP8X4), lhsT_scale=eg_s[:, cols],
                                     rhs=w1_c[:].bitcast(FP8X4), rhs_scale=w1_s[:], start=True, stop=True)
                 y_sb = reuse.tile([P, H], F32, name=f"yT{h}{g}", align_bytes=64, offset=4096 + 2048 * (2 * h + g))
                 nc.scalar.activation(y_sb[:], pb[:], ACT.Copy, scale=c_t[:, 2 * h + g : 2 * h + g + 1])
                 yT.append(y_sb)
-            pa = []
+            ax = sb.tile([P, 4, HALF], F32, name=f"ax{h}")
+            hx = sb.tile([P, 4, HALF], F32, name=f"hx{h}")
+            pa, y = [], []
             for u in range(2):
-                bank = ps.tile([P, 2, HALF], F32, name=f"pa{h}{u}", tag=f"pa{h}", bufs=2)
+                bank = ps.tile([P, 2, HALF], F32, name=f"pa{h}{u}", tag=pa_tags[u])
                 for tt in range(2):
                     cols = slice(P * (2 * u + tt), P * (2 * u + tt + 1))
                     nc.tensor.matmul_mx(out=bank[:, tt, :], lhsT=w1_c[:, cols].bitcast(FP8X4), lhsT_scale=w1_s[:, cols],
                                         rhs=xg_w[:].bitcast(FP8X4), rhs_scale=xg_s, start=True, stop=True)
+                for tt in range(2):
+                    t = 2 * u + tt
+                    nc.scalar.activation(ax[:, t, :], bank[:, tt, :], ACT.Copy, scale=cross[:, t : t + 1])
                 pa.append(bank)
-            ax = sb.tile([P, 4, HALF], F32, name=f"ax{h}")
-            hx = sb.tile([P, 4, HALF], F32, name=f"hx{h}")
-            for t in range(4):
-                nc.scalar.activation(ax[:, t, :], pa[t // 2][:, t % 2, :], ACT.Copy, scale=cross[:, t : t + 1])
-            for t in range(4):
-                nc.scalar.activation(hx[:, t, :], pa[t // 2][:, t % 2, :], ACT.Square, scale=root[:, t : t + 1])
-            y = []
-            for u in range(2):
-                bank = ps.tile([P, 2, HALF], F32, name=f"y{h}{u}", tag="y" if h == 0 else "pa0", bufs=2)
+                bank = ps.tile([P, 2, HALF], F32, name=f"y{h}{u}", tag=y_tags[u])
                 for g in range(2):
                     for tt in range(2):
                         t = 2 * u + tt
                         nc.tensor.transpose(bank[:, tt, P * g : P * (g + 1)], yT[g][:, P * t : P * (t + 1)], ident[:])
                 y.append(bank)
+            for t in range(4):
+                nc.scalar.activation(hx[:, t, :], pa[t // 2][:, t % 2, :], ACT.Square, scale=root[:, t : t + 1])
             return ax, hx, y
 
         fronts = [front(h) for h in range(2)]
@@ -198,7 +195,7 @@ def tile_picked_yplda_quad_p_kernel(
             return zz_c, zz_s
 
         def finish(h, zq, j0, n, tag, queue):
-            acc = ps.tile([P, n], F32, name=f"acc{h}_{j0}", tag=tag, bufs=2)
+            acc = ps.tile([P, n], F32, name=f"acc{h}_{j0}", tag=tag)
             nc.tensor.matmul_mx(out=acc[:], lhsT=wo_c[:].bitcast(FP8X4), lhsT_scale=wo_s[:],
                                 rhs=zq[0][:].bitcast(FP8X4), rhs_scale=zq[1][:], start=True, stop=True)
             res = sb.tile([P, n], F32, name=f"res{h}_{j0}")
@@ -211,7 +208,7 @@ def tile_picked_yplda_quad_p_kernel(
         zq0 = quantised(0, zz0, 0, HALF)
         zz1a = rounded(1, prod1, 0, P)
         nc.vector.quantize_mx(out=wo_c[:].bitcast(FP8X4), scales=wo_s[:], in_=wo_b[:].rearrange("p n j -> p (n j)"))
-        finish(0, zq0, 0, HALF, "y", nc.sync)
+        finish(0, zq0, 0, HALF, "D", nc.sync)
         zz1b = rounded(1, prod1, P, P)
-        finish(1, quantised(1, zz1a, 0, P), 0, P, "y", nc.sync)
-        finish(1, quantised(1, zz1b, P, P), P, P, "pb", nc.scalar)
+        finish(1, quantised(1, zz1a, 0, P), 0, P, "E", nc.sync)
+        finish(1, quantised(1, zz1b, P, P), P, P, "F", nc.scalar)

from contextlib import ExitStack

import concourse.mybir as mybir
from concourse.masks import make_identity

F32 = mybir.dt.float32
BF16 = mybir.dt.bfloat16
I32 = mybir.dt.int32
U32 = mybir.dt.uint32
U16 = mybir.dt.uint16
U8 = mybir.dt.uint8
FP8X4 = mybir.dt.float8_e4m3fn_x4
ALU = mybir.AluOpType
ACT = mybir.ActivationFunctionType

P = 128
K, T, S, H, N = 512, 1024, 512, 512, 128
FLOPS = 2 * K * H * S * 2 + 2 * H * N * S
HALF = S // 2


def tile_picked_yplda_quad_p_kernel(
    tc, x_words, x_scales, w1, e_words, e_scales, cond, across, within, unit, wo, offs, test, out
):
    nc = tc.nc
    with ExitStack() as ctx:
        sb = ctx.enter_context(tc.tile_pool(name="sb", bufs=1))
        ps = ctx.enter_context(tc.psum_pool(name="ps", bufs=1))
        reuse = ctx.enter_context(tc.tile_pool(name="reuse", bufs=1))

        offs_t = sb.tile([P, S // 16], U16, name="offs_t")
        test_t = sb.tile([P, S // 16], U16, name="test_t")
        xw_win = sb.tile([P, T], I32, name="xw_win", align_bytes=64)
        ew_win = sb.tile([P, T], I32, name="ew_win", align_bytes=64)
        xs_win = sb.tile([P, T], U8, name="xs_win", align_bytes=64)
        es_win = sb.tile([P, T], U8, name="es_win", align_bytes=64)
        w1_raw = [sb.tile([P, 4, H // 2], F32, name=f"w1_raw{u}") for u in range(2)]
        wo_raw = sb.tile([P, 4, N], F32, name="wo_raw")
        a_t = sb.tile([P, 4], F32, name="a_t")
        w_t = sb.tile([P, 4], F32, name="w_t")
        u_t = sb.tile([P, 4], F32, name="u_t")
        c_t = sb.tile([P, 4], F32, name="c_t")

        def load_scales(win, src):
            for q in range(4):
                rows = src[0:1, 4 * q : 4 * q + 4, :].bitcast(I32)
                nc.sync.dma_start(win[32 * q : 32 * q + 32, :].bitcast(I32), rows.broadcast_to([8, 4, T // 4]))

        nc.gpsimd.memset(xs_win[:].bitcast(I32), 0)
        w1v = w1.rearrange("(p j) c -> p j c", j=4)
        nc.sync.dma_start(w1_raw[0][:], w1v[:, :, 0:256])
        nc.sync.dma_start(test_t[:], test)
        load_scales(es_win, e_scales)
        nc.sync.dma_start(w1_raw[1][:], w1v[:, :, 256:512])
        nc.sync.dma_start(ew_win[:], e_words[0].rearrange("p n t -> p (n t)").bitcast(I32))
        nc.sync.dma_start(xw_win[:], x_words[0].rearrange("p n t -> p (n t)").bitcast(I32))
        nc.sync.dma_start(offs_t[:], offs)
        with nc.allow_non_contiguous_dma(reason="one factor a pair, pairs on the partitions"):
            nc.sync.dma_start(c_t[:], cond[0:1, :].rearrange("o (g p) -> p (o g)", p=P))
        for q in range(4):
            nc.sync.dma_start(xs_win[32 * q : 32 * q + 4, :].bitcast(I32), x_scales[0, 4 * q : 4 * q + 4, :].bitcast(I32))
        nc.sync.dma_start(wo_raw[:], wo.rearrange("(p j) n -> p j n", j=4))
        for tl, src in ((u_t, unit), (w_t, within), (a_t, across)):
            nc.gpsimd.dma_start(tl[:], src.rearrange("(p t) o -> p (t o)", t=4))

        cross = sb.tile([P, 4], F32, name="cross")
        uw = sb.tile([P, 4], F32, name="uw")
        nsq = sb.tile([P, 4], F32, name="nsq")
        ident = sb.tile([P, P], F32, name="ident")
        make_identity(nc, ident[:])
        ua = sb.tile([P, 4], F32, name="ua")
        ua2 = sb.tile([P, 4], F32, name="ua2")
        s5 = sb.tile([P, 4], F32, name="s5")
        root = sb.tile([P, 4], F32, name="root")
        half = sb.tile([P, 4], F32, name="half")
        nc.gpsimd.memset(half[:], 0.5)
        nc.gpsimd.tensor_tensor(uw[:], u_t[:], w_t[:], ALU.mult)
        nc.gpsimd.tensor_scalar(s5[:], uw[:], 0.0, -0.5, ALU.is_ge, ALU.add)
        nc.gpsimd.tensor_tensor(ua[:], u_t[:], a_t[:], ALU.mult)
        nc.gpsimd.tensor_scalar(ua2[:], s5[:], -2.0, 0.0, ALU.mult, ALU.add)
        nc.gpsimd.tensor_tensor(nsq[:], uw[:], s5[:], ALU.mult)
        nc.gpsimd.tensor_tensor(cross[:], ua[:], ua2[:], ALU.mult)
        nc.gpsimd.tensor_tensor(root[:], nsq[:], half[:], ALU.pow)

        def gather_scales(name, win, lst):
            g_s = sb.tile([P, S], U8, name=name, align_bytes=64)
            nc.vector.tensor_copy(g_s[:], win[:].indirect(lst[:]))
            return g_s

        def gather_words(name, win, lst, h, base):
            g_w = reuse.tile([P, HALF], U32, name=f"{name}{h}", align_bytes=64, offset=base)
            nc.vector.tensor_copy(g_w[:], win[:].bitcast(U32).indirect(lst[:, h * 16 : (h + 1) * 16]))
            return g_w

        eg_sc = gather_scales("eg_s", es_win, test_t)

        w1_b = reuse.tile([P, 4, P, 4], BF16, name="w1_b", align_bytes=64, offset=0)

        def cast_w1(copy, u, m0, m1):
            src = w1_raw[u][:, :, 4 * m0 : 4 * m1].rearrange("p j (m t) -> p m j t", t=4)
            dst = w1_b[:, :, 64 * u + m0 : 64 * u + m1, :].rearrange("p t m j -> p m j t")
            copy(dst, src)

        cast_w1(nc.scalar.copy, 0, 0, 64)
        cast_w1(nc.scalar.copy, 1, 0, 20)
        cast_w1(nc.vector.tensor_copy, 1, 20, 64)
        w1_c = sb.tile([P, H], U32, name="w1_c", align_bytes=64)
        w1_s = sb.tile([P, H], U8, name="w1_s", align_bytes=64)
        nc.vector.quantize_mx(out=w1_c[:].bitcast(FP8X4), scales=w1_s[:], in_=w1_b[:].rearrange("p t m j -> p (t m j)"))

        eg = [(gather_words("eg_w", ew_win, test_t, h, 1024 * h), eg_sc[:, h * HALF : (h + 1) * HALF]) for h in range(2)]
        xg = []
        for h in range(2):
            words = gather_words("xg_w", xw_win, offs_t, h, 2048 + 1024 * h)
            g_s = sb.tile([P, HALF], U8, name=f"xg_s{h}", align_bytes=64)
            nc.vector.tensor_copy(g_s[:], xs_win[:].indirect(offs_t[:, h * 16 : (h + 1) * 16]))
            xg.append((words, g_s[:]))

        wo_b = sb.tile([P, N, 4], BF16, name="wo_b", align_bytes=64)
        wo_c = sb.tile([P, N], U32, name="wo_c", align_bytes=64)
        wo_s = sb.tile([P, N], U8, name="wo_s", align_bytes=64)


        def front(h):
            eg_w, eg_s = eg[h]
            xg_w, xg_s = xg[h]
            pb_tags, pa_tags, y_tags = (("AB", "CB", "DE"), ("AF", "GH", "CA"))[h]
            yT = []
            for g in range(2):
                pb = ps.tile([P, H], F32, name=f"pb{h}{g}", tag=pb_tags[g])
                cols = slice(P * g, P * (g + 1))
                nc.tensor.matmul_mx(out=pb[:], lhsT=eg_w[:, cols].bitcast(FP8X4), lhsT_scale=eg_s[:, cols],
                                    rhs=w1_c[:].bitcast(FP8X4), rhs_scale=w1_s[:], start=True, stop=True)
                y_sb = reuse.tile([P, H], F32, name=f"yT{h}{g}", align_bytes=64, offset=4096 + 2048 * (2 * h + g))
                nc.scalar.activation(y_sb[:], pb[:], ACT.Copy, scale=c_t[:, 2 * h + g : 2 * h + g + 1])
                yT.append(y_sb)
            ax = sb.tile([P, 4, HALF], F32, name=f"ax{h}")
            hx = sb.tile([P, 4, HALF], F32, name=f"hx{h}")
            pa, y = [], []
            for u in range(2):
                bank = ps.tile([P, 2, HALF], F32, name=f"pa{h}{u}", tag=pa_tags[u])
                for tt in range(2):
                    cols = slice(P * (2 * u + tt), P * (2 * u + tt + 1))
                    nc.tensor.matmul_mx(out=bank[:, tt, :], lhsT=w1_c[:, cols].bitcast(FP8X4), lhsT_scale=w1_s[:, cols],
                                        rhs=xg_w[:].bitcast(FP8X4), rhs_scale=xg_s, start=True, stop=True)
                for tt in range(2):
                    t = 2 * u + tt
                    nc.scalar.activation(ax[:, t, :], bank[:, tt, :], ACT.Copy, scale=cross[:, t : t + 1])
                pa.append(bank)
                bank = ps.tile([P, 2, HALF], F32, name=f"y{h}{u}", tag=y_tags[u])
                for g in range(2):
                    for tt in range(2):
                        t = 2 * u + tt
                        nc.tensor.transpose(bank[:, tt, P * g : P * (g + 1)], yT[g][:, P * t : P * (t + 1)], ident[:])
                y.append(bank)
            for t in range(4):
                nc.scalar.activation(hx[:, t, :], pa[t // 2][:, t % 2, :], ACT.Square, scale=root[:, t : t + 1])
            return ax, hx, y

        fronts = [front(h) for h in range(2)]
        wo_sg = reuse.tile([P, 4, N], F32, name="wo_sg", align_bytes=64, offset=4096 + 2048 * 3)
        for j in range(4):
            nc.scalar.activation(wo_sg[:, j, :], wo_raw[:, j, :], ACT.Copy, scale=ua2[:, j : j + 1])
        nc.scalar.copy(wo_b[:].rearrange("p (c i) j -> p c j i", i=4), wo_sg[:].rearrange("p j (c i) -> p c j i", i=4))

        def linear(h):
            ax, hx, y = fronts[h]
            lin = sb.tile([P, 4, HALF], F32, name=f"lin{h}")
            for t in range(4):
                nc.vector.scalar_tensor_tensor(lin[:, t, :], y[t // 2][:, t % 2, :], nsq[:, t : t + 1], ax[:, t, :], ALU.mult, ALU.add)
            return lin

        def products(h, lin):
            y = fronts[h][2]
            prod = sb.tile([P, 4, HALF], F32, name=f"prod{h}")
            for u in range(2):
                nc.vector.tensor_tensor(prod[:, 2 * u : 2 * u + 2, :], y[u][:], lin[:, 2 * u : 2 * u + 2, :], ALU.mult)
            return prod

        def rounded(h, prod, j0, n):
            hx = fronts[h][1]
            zz = sb.tile([P, n, 4], BF16, name=f"zz{h}_{j0}", align_bytes=64)
            nc.vector.tensor_tensor(
                zz[:].rearrange("p (c i) t -> p c t i", i=4),
                prod[:, :, j0 : j0 + n].rearrange("p t (c i) -> p c t i", i=4),
                hx[:, :, j0 : j0 + n].rearrange("p t (c i) -> p c t i", i=4),
                ALU.add,
            )
            return zz

        def quantised(h, zz, j0, n):
            zz_c = sb.tile([P, n], U32, name=f"zz_c{h}_{j0}", align_bytes=64)
            zz_s = sb.tile([P, n], U8, name=f"zz_s{h}_{j0}", align_bytes=64)
            nc.vector.quantize_mx(out=zz_c[:].bitcast(FP8X4), scales=zz_s[:], in_=zz[:].rearrange("p j t -> p (j t)"))
            return zz_c, zz_s

        def finish(h, zq, j0, n, tag, queue):
            acc = ps.tile([P, n], F32, name=f"acc{h}_{j0}", tag=tag)
            nc.tensor.matmul_mx(out=acc[:], lhsT=wo_c[:].bitcast(FP8X4), lhsT_scale=wo_s[:],
                                rhs=zq[0][:].bitcast(FP8X4), rhs_scale=zq[1][:], start=True, stop=True)
            res = sb.tile([P, n], F32, name=f"res{h}_{j0}")
            nc.scalar.copy(res[:], acc[:])
            queue.dma_start(out[:, h * HALF + j0 : h * HALF + j0 + n], res[:])

        prod0 = products(0, linear(0))
        zz0 = rounded(0, prod0, 0, HALF)
        prod1 = products(1, linear(1))
        zq0 = quantised(0, zz0, 0, HALF)
        zz1a = rounded(1, prod1, 0, P)
        nc.vector.quantize_mx(out=wo_c[:].bitcast(FP8X4), scales=wo_s[:], in_=wo_b[:].rearrange("p n j -> p (n j)"))
        finish(0, zq0, 0, HALF, "D", nc.sync)
        zz1b = rounded(1, prod1, P, P)
        finish(1, quantised(1, zz1a, 0, P), 0, P, "E", nc.sync)
        finish(1, quantised(1, zz1b, P, P), P, P, "F", nc.scalar)
